import numpy as np
import ml_dtypes


def mxq(x, axis, fmt="e4m3"):
    dtype, down = {"e4m3": (ml_dtypes.float8_e4m3fn, 7), "e5m2": (ml_dtypes.float8_e5m2, 14)}[fmt]
    v = np.moveaxis(np.asarray(x, np.float32).astype(ml_dtypes.bfloat16).astype(np.float64), axis, -1)
    blocks = v.reshape(v.shape[:-1] + (-1, 32))
    amax = np.abs(blocks).max(-1, keepdims=True)
    byte = np.maximum(np.where(amax > 0, np.frexp(amax)[1] - 1 + 127, 0) - down, 1)
    scale = np.exp2(byte - 127.0)
    codes = (blocks / scale).astype(np.float32).astype(dtype).astype(np.float64)
    return np.moveaxis((codes * scale).reshape(v.shape), -1, axis)


WIDE = False


def mx_kscale(k):
    if not WIDE:
        return np.ones(k)
    levels = np.array([10, -10, 5, -5, 0])
    if k % 512:
        return np.exp2(np.random.permutation(np.resize(levels, k // 32))).repeat(32)
    a = np.empty((k // 512, 16))
    for p in range(k // 512):
        a[p, :8] = np.random.permutation(np.resize(levels, 8))
        for g in range(8):
            far = levels[np.abs(levels - a[p, g]) >= 10]
            a[p, g + 8] = far[np.random.randint(len(far))]
    return np.exp2(a.ravel()).repeat(32)


def f64(x):
    return np.asarray(x).astype(np.float64)


def striped8(idx):
    return np.asarray(idx).reshape(8, -1, 16).transpose(0, 2, 1).reshape(128, -1).astype(np.uint16)


def unstriped8(offs):
    return offs.reshape(8, 16, -1).transpose(0, 2, 1).reshape(8, -1).astype(np.int64)


def pick8(x, idx, run):
    r = np.arange(len(x))
    return x[r[:, None], idx[r % (8 * run) // run]]


E2M1 = np.array([0.0, 0.5, 1.0, 1.5, 2.0, 3.0, 4.0, 6.0, -0.0, -0.5, -1.0, -1.5, -2.0, -3.0, -4.0, -6.0])


def pack_weight(w, fmt):
    k, n = w.shape
    w = f64(np.asarray(w, np.float32).astype(ml_dtypes.bfloat16)).reshape(k // 32, 32, n)
    amax = np.abs(w).max(1)
    if fmt == "e4m3":
        byte = np.frexp(amax)[1] - 1 + 127 - 7
    else:
        mant, ex = np.frexp(amax / 6.0)
        byte = np.where(mant > 0.5, ex, ex - 1) + 127
    byte = np.clip(np.where(amax > 0, byte, 1), 1, 254)
    scaled = (w * np.exp2(127.0 - byte)[:, None, :]).reshape(k, n).astype(np.float32)
    by_word = np.ascontiguousarray(scaled.reshape(k // 512, 128, 4, n).transpose(0, 1, 3, 2))
    if fmt == "e4m3":
        words = by_word.astype(ml_dtypes.float8_e4m3fn).view(np.uint8)
    else:
        c = by_word.astype(ml_dtypes.float4_e2m1fn).view(np.uint8) & 0xF
        words = (c[..., 0::2] | (c[..., 1::2] << 4)).reshape(k // 512, 128, 2 * n)
    return np.ascontiguousarray(words), np.ascontiguousarray(byte.astype(np.uint8).reshape(k // 512, 16, n))


def unpack_weight(words, scales, fmt):
    g, _, n = scales.shape
    words = np.ascontiguousarray(words).reshape(g, 128, n, -1)
    if fmt == "e4m3":
        vals = words.view(ml_dtypes.float8_e4m3fn).astype(np.float64)
    else:
        nib = np.empty((g, 128, n, 4), np.uint8)
        nib[..., 0::2] = words & 0xF
        nib[..., 1::2] = words >> 4
        vals = E2M1[nib]
    vals = vals * np.repeat(np.exp2(scales.astype(np.float64) - 127.0), 8, axis=1)[..., None]
    return vals.transpose(0, 1, 3, 2).reshape(g * 512, n)


def softplus(v):
    return np.log(1.0 + np.exp(v))


D, T, I, Q = 512, 1024, 512, 128


def setup_inputs():
    n = np.random.standard_normal
    idx = np.stack([np.random.permutation(T)[:I] for _ in range(8)])
    idx2 = np.stack([np.random.permutation(T)[:I] for _ in range(8)])
    idx3 = np.stack([np.random.permutation(T)[:I] for _ in range(8)])
    fd = mx_kscale(D)
    keysp = pack_weight(n((D, T)) / fd[:, None], "e4m3")
    return {
        "query": (n((D, Q)) * 0.9 / np.sqrt(D) * fd[:, None]).astype(np.float32),
        "query2": (n((D, Q)) * 0.9 / np.sqrt(D) * fd[:, None]).astype(np.float32),
        "keys_words": keysp[0],
        "keys_scales": keysp[1],
        "lam": (np.random.uniform(0.6, 1.2, (Q, 1))).astype(np.float32),
        "old": (1.0 * n((Q, T))).astype(np.float32),
        "offs": striped8(idx),
        "offs2": striped8(idx2),
        "offs3": striped8(idx3),
    }


def reference(query, query2, keys_words, keys_scales, lam, old, offs, offs2, offs3):
    idx = unstriped8(offs)
    idx2 = unstriped8(offs2)
    idx3 = unstriped8(offs3)
    keysu = unpack_weight(keys_words, keys_scales, "e4m3")
    queryq = mxq(f64(query), 0, "e4m3")
    a = queryq.T @ keysu
    query2q = mxq(f64(query2), 0, "e4m3")
    b = query2q.T @ keysu
    w = pick8(a, idx, 16) / (softplus(pick8(b, idx2, 16)) + 0.5) * f64(lam)
    f1 = np.zeros((Q, T))
    f1[np.arange(Q)[:, None], idx[np.arange(Q) % 128 // 16]] = w
    f2 = f1 + f64(old)
    y = pick8(f2, idx3, 16)
    return y

@@ -1,0 +1,144 @@
+import math
+from contextlib import ExitStack
+
+import concourse.mybir as mybir
+
+D, T, I, Q = 512, 1024, 512, 128
+P = 128
+PACK = 4
+FLOPS = 2 * 2 * D * Q * T
+
+F32 = mybir.dt.float32
+BF16 = mybir.dt.bfloat16
+I32 = mybir.dt.int32
+U32 = mybir.dt.uint32
+U16 = mybir.dt.uint16
+U8 = mybir.dt.uint8
+FP8X4 = mybir.dt.float8_e4m3fn_x4
+ALU = mybir.AluOpType
+ACT = mybir.ActivationFunctionType
+
+FLOOR_AT = 40.0
+NV = 160
+NB = 256
+
+
+def tile_attend_worthfor_lean_through_heads_kernel(
+    tc, query, query2, keys_words, keys_scales, lam, old, offs, offs2, offs3, out
+):
+    nc = tc.nc
+    with ExitStack() as ctx:
+        keep = ctx.enter_context(tc.tile_pool(name="keep", bufs=1))
+        psum = ctx.enter_context(tc.psum_pool(name="psum", bufs=1))
+
+        def cols(lo, n):
+            return slice(lo // 16, (lo + n) // 16)
+
+        raw2 = keep.tile([P, PACK, Q], F32, name="raw2")
+        nc.sync.dma_start(out=raw2[:], in_=query2.rearrange("(p j) q -> p j q", j=PACK))
+        kscale = keep.tile([P, T], U8, name="kscale", align_bytes=64)
+        for g in range(4):
+            (nc.sync if g < 2 else nc.scalar).dma_start(
+                out=kscale[32 * g : 32 * g + 4, :].bitcast(I32),
+                in_=keys_scales[0, 4 * g : 4 * g + 4, :].bitcast(I32),
+            )
+        words = keys_words[0].rearrange("p n t -> p (n t)")
+        kw = []
+        for h in range(2):
+            t = keep.tile([P, T // 2], U32, name=f"kw{h}", align_bytes=64)
+            nc.sync.dma_start(out=t[:].bitcast(I32), in_=words[:, h * 2 * T : (h + 1) * 2 * T].bitcast(I32))
+            kw.append(t)
+        raw1 = keep.tile([P, PACK, Q], F32, name="raw1")
+        nc.sync.dma_start(out=raw1[:], in_=query.rearrange("(p j) q -> p j q", j=PACK))
+        o2 = keep.tile([P, I // 16], U16, name="o2")
+        nc.sync.dma_start(o2[:], offs2)
+        o1 = keep.tile([P, I // 16], U16, name="o1")
+        nc.sync.dma_start(o1[:], offs)
+        o3 = keep.tile([P, I // 16], U16, name="o3")
+        nc.sync.dma_start(o3[:], offs3)
+        lam_t = keep.tile([P, 1], F32, name="lam_t")
+        nc.sync.dma_start(out=lam_t[:], in_=lam)
+        old_t = keep.tile([P, T], F32, name="old_t")
+        nc.sync.dma_start(out=old_t[:], in_=old)
+
+        floor_arg = keep.tile([P, 1], F32, name="floor_arg")
+        nc.vector.memset(floor_arg[:], -FLOOR_AT)
+        half = keep.tile([P, 1], F32, name="half")
+        nc.vector.memset(half[:], 0.5)
+        floor = keep.tile([P, 1], F32, name="floor")
+        nc.scalar.activation(floor[:], floor_arg[:], ACT.Sigmoid)
+        f1 = keep.tile([P, T], F32, name="f1")
+        nc.vector.memset(f1[:], 0.0)
+
+        def quantise(name, raw):
+            g = keep.tile([P, Q, PACK], BF16, name=name + "_g", align_bytes=64)
+            nc.vector.tensor_copy(
+                out=g[:].rearrange("p (c i) t -> p c t i", i=4), in_=raw[:].rearrange("p t (c i) -> p c t i", i=4)
+            )
+            c = keep.tile([P, Q], U32, name=name + "_c", align_bytes=64)
+            s = keep.tile([P, Q], U8, name=name + "_s", align_bytes=64)
+            nc.vector.quantize_mx(out=c[:].bitcast(FP8X4), scales=s[:], in_=g[:].rearrange("p q t -> p (q t)"))
+            return c, s
+
+        def product(name, codes, scales, lo, n):
+            bank = psum.tile([P, n], F32, name=name)
+            h, off = divmod(lo, T // 2)
+            nc.tensor.matmul_mx(
+                out=bank[:],
+                lhsT=codes[:].bitcast(FP8X4),
+                lhsT_scale=scales[:],
+                rhs=kw[h][:, off : off + n].bitcast(FP8X4),
+                rhs_scale=kscale[:, lo : lo + n],
+                start=True,
+                stop=True,
+            )
+            return bank
+
+        c2, s2 = quantise("q2", raw2)
+        b = keep.tile([P, T], F32, name="b")
+        for j in range(T // NB):
+            bank = product(f"b{j}", c2, s2, j * NB, NB)
+            nc.scalar.copy(out=b[:, j * NB : (j + 1) * NB], in_=bank[:])
+        c1, s1 = quantise("q1", raw1)
+        abanks = [product(f"a{j}", c1, s1, j * 512, 512) for j in range(2)]
+
+        H = I // 2
+        nb = keep.tile([P, I], F32, name="nb")
+        sg = keep.tile([P, I], F32, name="sg")
+        nc.scalar.activation(sg[:, H:], b[:].indirect(o2[:, cols(H, H)]), ACT.Sigmoid, scale=-1.0)
+        nc.vector.tensor_scalar(nb[:, :H], b[:].indirect(o2[:, cols(0, H)]), -1.0, -0.5, ALU.mult, ALU.add)
+        nc.scalar.activation(sg[:, :H], nb[:, :H], ACT.Sigmoid, bias=half[:])
+        nc.vector.tensor_scalar(nb[:, H:], b[:].indirect(o2[:, cols(H, H)]), -1.0, -0.5, ALU.mult, ALU.add)
+        a = keep.tile([P, T], F32, name="a")
+        for j in range(2):
+            nc.vector.tensor_copy(out=a[:, j * 512 : (j + 1) * 512], in_=abanks[j][:])
+        lg = keep.tile([P, I], F32, name="lg")
+        nd = keep.tile([P, I], F32, name="nd")
+        ag = keep.tile([P, I], F32, name="ag")
+        al = keep.tile([P, NV], F32, name="al")
+        rs = keep.tile([P, I], F32, name="rs")
+        r = keep.tile([P, I], F32, name="r")
+        sv, ss = slice(0, NV), slice(NV, I)
+        for s in (sv, ss):
+            nc.scalar.activation(lg[:, s], sg[:, s], ACT.Ln, scale=math.exp(-0.5), bias=floor[:])
+        sq = rs[:, NV : 2 * NV]
+        nc.vector.tensor_copy(ag[:, :H], a[:].indirect(o1[:, cols(0, H)]))
+        nc.vector.tensor_tensor(nd[:, sv], nb[:, sv], lg[:, sv], ALU.min)
+        nc.vector.tensor_tensor(sq, nd[:, sv], nd[:, sv], ALU.mult)
+        nc.vector.tensor_tensor(nd[:, ss], nb[:, ss], lg[:, ss], ALU.min)
+        nc.vector.tensor_scalar(al[:], ag[:, sv], lam_t[:], None, ALU.mult)
+        nc.vector.tensor_copy(ag[:, H:], a[:].indirect(o1[:, cols(H, H)]))
+        nc.scalar.activation(r[:, sv], sq, ACT.Abs_reciprocal_sqrt)
+        nc.vector.tensor_tensor(f1[:].indirect(o1[:, cols(0, NV)]), al[:], r[:, sv], ALU.mult)
+        nc.scalar.activation(rs[:, ss], nd[:, ss], ACT.Abs_reciprocal_sqrt)
+        nc.scalar.activation(r[:, ss], rs[:, ss], ACT.Square)
+        nc.scalar.activation(rs[:, ss], r[:, ss], ACT.Copy, scale=lam_t[:])
+        nc.vector.tensor_tensor(f1[:].indirect(o1[:, cols(NV, I - NV)]), ag[:, ss], rs[:, ss], ALU.mult)
+        f2 = keep.tile([P, T], F32, name="f2")
+        nc.vector.tensor_tensor(f2[:], f1[:], old_t[:], ALU.add)
+        y0 = keep.tile([P, H], F32, name="y0")
+        y1 = keep.tile([P, H], F32, name="y1")
+        nc.vector.tensor_copy(y0[:], f2[:].indirect(o3[:, cols(0, H)]))
+        nc.scalar.activation(y1[:], f2[:].indirect(o3[:, cols(H, H)]), ACT.Copy)
+        nc.sync.dma_start(out=out[:, :H], in_=y0[:])
+        nc.scalar.dma_start(out=out[:, H:], in_=y1[:])

@@ -19,7 +19,7 @@ ALU = mybir.AluOpType
 ACT = mybir.ActivationFunctionType
 
 FLOOR_AT = 40.0
-NV = 160
+NV = 224
 NB = 256
 
 
@@ -72,12 +72,18 @@ def tile_attend_worthfor_lean_through_heads_kernel(
 
         def quantise(name, raw):
             g = keep.tile([P, Q, PACK], BF16, name=name + "_g", align_bytes=64)
-            nc.vector.tensor_copy(
-                out=g[:].rearrange("p (c i) t -> p c t i", i=4), in_=raw[:].rearrange("p t (c i) -> p c t i", i=4)
-            )
+            halves = (slice(0, Q // 2), slice(Q // 2, Q))
+            for hs in halves:
+                nc.vector.tensor_copy(
+                    out=g[:, hs, :].rearrange("p (c i) t -> p c t i", i=4),
+                    in_=raw[:, :, hs].rearrange("p t (c i) -> p c t i", i=4),
+                )
             c = keep.tile([P, Q], U32, name=name + "_c", align_bytes=64)
             s = keep.tile([P, Q], U8, name=name + "_s", align_bytes=64)
-            nc.vector.quantize_mx(out=c[:].bitcast(FP8X4), scales=s[:], in_=g[:].rearrange("p q t -> p (q t)"))
+            for hs in halves:
+                nc.vector.quantize_mx(
+                    out=c[:, hs].bitcast(FP8X4), scales=s[:, hs], in_=g[:, hs, :].rearrange("p q t -> p (q t)")
+                )
             return c, s
 
         def product(name, codes, scales, lo, n):

@@ -2,6 +2,7 @@ import math
 from contextlib import ExitStack
 
 import concourse.mybir as mybir
+from concourse.masks import make_identity
 
 D, T, I, Q = 512, 1024, 512, 128
 P = 128
@@ -21,6 +22,7 @@ ACT = mybir.ActivationFunctionType
 FLOOR_AT = 40.0
 NV = 224
 NB = 256
+ADD_V = 640
 
 
 def tile_attend_worthfor_lean_through_heads_kernel(
@@ -69,6 +71,9 @@ def tile_attend_worthfor_lean_through_heads_kernel(
         nc.scalar.activation(floor[:], floor_arg[:], ACT.Sigmoid)
         f1 = keep.tile([P, T], F32, name="f1")
         nc.vector.memset(f1[:], 0.0)
+
+        ident = keep.tile([P, P], F32, name="ident")
+        make_identity(nc, ident[:])
 
         def quantise(name, raw):
             g = keep.tile([P, Q, PACK], BF16, name=name + "_g", align_bytes=64)
@@ -123,7 +128,7 @@ def tile_attend_worthfor_lean_through_heads_kernel(
         ag = keep.tile([P, I], F32, name="ag")
         al = keep.tile([P, NV], F32, name="al")
         rs = keep.tile([P, I], F32, name="rs")
-        r = keep.tile([P, I], F32, name="r")
+        r = keep.tile([P, NV], F32, name="r")
         sv, ss = slice(0, NV), slice(NV, I)
         for s in (sv, ss):
             nc.scalar.activation(lg[:, s], sg[:, s], ACT.Ln, scale=math.exp(-0.5), bias=floor[:])
@@ -137,11 +142,24 @@ def tile_attend_worthfor_lean_through_heads_kernel(
         nc.scalar.activation(r[:, sv], sq, ACT.Abs_reciprocal_sqrt)
         nc.vector.tensor_tensor(f1[:].indirect(o1[:, cols(0, NV)]), al[:], r[:, sv], ALU.mult)
         nc.scalar.activation(rs[:, ss], nd[:, ss], ACT.Abs_reciprocal_sqrt)
-        nc.scalar.activation(r[:, ss], rs[:, ss], ACT.Square)
-        nc.scalar.activation(rs[:, ss], r[:, ss], ACT.Copy, scale=lam_t[:])
+        turned = keep.tile([P, ADD_V], F32, name="turned")
+        r2 = turned[:, ADD_V - (I - NV) :]
+        nc.scalar.activation(r2, rs[:, ss], ACT.Square)
+        nc.scalar.activation(rs[:, ss], r2, ACT.Copy, scale=lam_t[:])
         nc.vector.tensor_tensor(f1[:].indirect(o1[:, cols(NV, I - NV)]), ag[:, ss], rs[:, ss], ALU.mult)
         f2 = keep.tile([P, T], F32, name="f2")
-        nc.vector.tensor_tensor(f2[:], f1[:], old_t[:], ALU.add)
+        pieces = ((0, 512), (512, ADD_V - 512))
+        for j, (lo, n) in enumerate(pieces):
+            bank = psum.tile([P, n], F32, name=f"t{j}", tag=f"a{j}")
+            for c in range(0, n, P):
+                nc.tensor.transpose(bank[:, c : c + P], old_t[:, lo + c : lo + c + P], ident[:])
+            nc.scalar.copy(out=turned[:, lo : lo + n], in_=bank[:])
+        nc.gpsimd.tensor_tensor(f2[:, ADD_V:], f1[:, ADD_V:], old_t[:, ADD_V:], ALU.add)
+        for j, (lo, n) in enumerate(pieces):
+            bank = psum.tile([P, n], F32, name=f"u{j}", tag=f"b{2 + j}")
+            for c in range(0, n, P):
+                nc.tensor.transpose(bank[:, c : c + P], turned[:, lo + c : lo + c + P], ident[:])
+            nc.vector.tensor_tensor(f2[:, lo : lo + n], f1[:, lo : lo + n], bank[:], ALU.add)
         y0 = keep.tile([P, H], F32, name="y0")
         y1 = keep.tile([P, H], F32, name="y1")
         nc.vector.tensor_copy(y0[:], f2[:].indirect(o3[:, cols(0, H)]))

@@ -38,11 +38,11 @@ def tile_attend_worthfor_lean_through_heads_kernel(
 
         raw2 = keep.tile([P, PACK, Q], F32, name="raw2")
         nc.sync.dma_start(out=raw2[:], in_=query2.rearrange("(p j) q -> p j q", j=PACK))
-        kscale = keep.tile([P, T], U8, name="kscale", align_bytes=64)
+        kscale = keep.tile([P, NB], U8, name="kscale", align_bytes=64)
         for g in range(4):
             (nc.sync if g < 2 else nc.scalar).dma_start(
-                out=kscale[32 * g : 32 * g + 4, :].bitcast(I32),
-                in_=keys_scales[0, 4 * g : 4 * g + 4, :].bitcast(I32),
+                out=kscale[32 * g : 32 * g + 16, :].bitcast(I32),
+                in_=keys_scales[0, 4 * g : 4 * g + 4, :].rearrange("r (j c) -> j r c", j=4).bitcast(I32),
             )
         words = keys_words[0].rearrange("p n t -> p (n t)")
         kw = []
@@ -91,27 +91,32 @@ def tile_attend_worthfor_lean_through_heads_kernel(
                 )
             return c, s
 
-        def product(name, codes, scales, lo, n):
-            bank = psum.tile([P, n], F32, name=name)
+        def product(dst, codes, scales, lo, n):
             h, off = divmod(lo, T // 2)
+            j, col = divmod(lo, NB)
             nc.tensor.matmul_mx(
-                out=bank[:],
+                out=dst,
                 lhsT=codes[:].bitcast(FP8X4),
                 lhsT_scale=scales[:],
                 rhs=kw[h][:, off : off + n].bitcast(FP8X4),
-                rhs_scale=kscale[:, lo : lo + n],
+                rhs_scale=kscale[4 * j : P, col : col + n],
                 start=True,
                 stop=True,
             )
-            return bank
 
         c2, s2 = quantise("q2", raw2)
         b = keep.tile([P, T], F32, name="b")
         for j in range(T // NB):
-            bank = product(f"b{j}", c2, s2, j * NB, NB)
+            bank = psum.tile([P, NB], F32, name=f"b{j}")
+            product(bank[:], c2, s2, j * NB, NB)
             nc.scalar.copy(out=b[:, j * NB : (j + 1) * NB], in_=bank[:])
         c1, s1 = quantise("q1", raw1)
-        abanks = [product(f"a{j}", c1, s1, j * 512, 512) for j in range(2)]
+        abanks = []
+        for j in range(2):
+            bank = psum.tile([P, 512], F32, name=f"a{j}")
+            for u in range(2):
+                product(bank[:, u * NB : (u + 1) * NB], c1, s1, j * 512 + u * NB, NB)
+            abanks.append(bank)
 
         H = I // 2
         nb = keep.tile([P, I], F32, name="nb")

import math
from contextlib import ExitStack

import concourse.mybir as mybir
from concourse.masks import make_identity

D, T, I, Q = 512, 1024, 512, 128
P = 128
PACK = 4
FLOPS = 2 * 2 * D * Q * T

F32 = mybir.dt.float32
BF16 = mybir.dt.bfloat16
I32 = mybir.dt.int32
U32 = mybir.dt.uint32
U16 = mybir.dt.uint16
U8 = mybir.dt.uint8
FP8X4 = mybir.dt.float8_e4m3fn_x4
ALU = mybir.AluOpType
ACT = mybir.ActivationFunctionType

FLOOR_AT = 40.0
NV = 224
NB = 256
ADD_V = 640


def tile_attend_worthfor_lean_through_heads_kernel(
    tc, query, query2, keys_words, keys_scales, lam, old, offs, offs2, offs3, out
):
    nc = tc.nc
    with ExitStack() as ctx:
        keep = ctx.enter_context(tc.tile_pool(name="keep", bufs=1))
        psum = ctx.enter_context(tc.psum_pool(name="psum", bufs=1))

        def cols(lo, n):
            return slice(lo // 16, (lo + n) // 16)

        raw2 = keep.tile([P, PACK, Q], F32, name="raw2")
        nc.sync.dma_start(out=raw2[:], in_=query2.rearrange("(p j) q -> p j q", j=PACK))
        kscale = keep.tile([P, NB], U8, name="kscale", align_bytes=64)
        for g in range(4):
            (nc.sync if g < 2 else nc.scalar).dma_start(
                out=kscale[32 * g : 32 * g + 16, :].bitcast(I32),
                in_=keys_scales[0, 4 * g : 4 * g + 4, :].rearrange("r (j c) -> j r c", j=4).bitcast(I32),
            )
        words = keys_words[0].rearrange("p n t -> p (n t)")
        kw = []
        for h in range(2):
            t = keep.tile([P, T // 2], U32, name=f"kw{h}", align_bytes=64)
            nc.sync.dma_start(out=t[:].bitcast(I32), in_=words[:, h * 2 * T : (h + 1) * 2 * T].bitcast(I32))
            kw.append(t)
        raw1 = keep.tile([P, PACK, Q], F32, name="raw1")
        nc.sync.dma_start(out=raw1[:], in_=query.rearrange("(p j) q -> p j q", j=PACK))
        o2 = keep.tile([P, I // 16], U16, name="o2")
        nc.sync.dma_start(o2[:], offs2)
        o1 = keep.tile([P, I // 16], U16, name="o1")
        nc.sync.dma_start(o1[:], offs)
        o3 = keep.tile([P, I // 16], U16, name="o3")
        nc.sync.dma_start(o3[:], offs3)
        lam_t = keep.tile([P, 1], F32, name="lam_t")
        nc.sync.dma_start(out=lam_t[:], in_=lam)
        old_t = keep.tile([P, T], F32, name="old_t")
        nc.sync.dma_start(out=old_t[:], in_=old)

        floor_arg = keep.tile([P, 1], F32, name="floor_arg")
        nc.vector.memset(floor_arg[:], -FLOOR_AT)
        half = keep.tile([P, 1], F32, name="half")
        nc.vector.memset(half[:], 0.5)
        floor = keep.tile([P, 1], F32, name="floor")
        nc.scalar.activation(floor[:], floor_arg[:], ACT.Sigmoid)
        f1 = keep.tile([P, T], F32, name="f1")
        nc.vector.memset(f1[:], 0.0)

        ident = keep.tile([P, P], F32, name="ident")
        make_identity(nc, ident[:])

        def quantise(name, raw):
            g = keep.tile([P, Q, PACK], BF16, name=name + "_g", align_bytes=64)
            halves = (slice(0, Q // 2), slice(Q // 2, Q))
            for hs in halves:
                nc.vector.tensor_copy(
                    out=g[:, hs, :].rearrange("p (c i) t -> p c t i", i=4),
                    in_=raw[:, :, hs].rearrange("p t (c i) -> p c t i", i=4),
                )
            c = keep.tile([P, Q], U32, name=name + "_c", align_bytes=64)
            s = keep.tile([P, Q], U8, name=name + "_s", align_bytes=64)
            for hs in halves:
                nc.vector.quantize_mx(
                    out=c[:, hs].bitcast(FP8X4), scales=s[:, hs], in_=g[:, hs, :].rearrange("p q t -> p (q t)")
                )
            return c, s

        def product(dst, codes, scales, lo, n):
            h, off = divmod(lo, T // 2)
            j, col = divmod(lo, NB)
            nc.tensor.matmul_mx(
                out=dst,
                lhsT=codes[:].bitcast(FP8X4),
                lhsT_scale=scales[:],
                rhs=kw[h][:, off : off + n].bitcast(FP8X4),
                rhs_scale=kscale[4 * j : P, col : col + n],
                start=True,
                stop=True,
            )

        c2, s2 = quantise("q2", raw2)
        b = keep.tile([P, T], F32, name="b")
        for j in range(T // NB):
            bank = psum.tile([P, NB], F32, name=f"b{j}")
            product(bank[:], c2, s2, j * NB, NB)
            nc.scalar.copy(out=b[:, j * NB : (j + 1) * NB], in_=bank[:])
        c1, s1 = quantise("q1", raw1)
        abanks = []
        for j in range(2):
            bank = psum.tile([P, 512], F32, name=f"a{j}")
            for u in range(2):
                product(bank[:, u * NB : (u + 1) * NB], c1, s1, j * 512 + u * NB, NB)
            abanks.append(bank)

        H = I // 2
        nb = keep.tile([P, I], F32, name="nb")
        sg = keep.tile([P, I], F32, name="sg")
        nc.scalar.activation(sg[:, H:], b[:].indirect(o2[:, cols(H, H)]), ACT.Sigmoid, scale=-1.0)
        nc.vector.tensor_scalar(nb[:, :H], b[:].indirect(o2[:, cols(0, H)]), -1.0, -0.5, ALU.mult, ALU.add)
        nc.scalar.activation(sg[:, :H], nb[:, :H], ACT.Sigmoid, bias=half[:])
        nc.vector.tensor_scalar(nb[:, H:], b[:].indirect(o2[:, cols(H, H)]), -1.0, -0.5, ALU.mult, ALU.add)
        a = keep.tile([P, T], F32, name="a")
        for j in range(2):
            nc.vector.tensor_copy(out=a[:, j * 512 : (j + 1) * 512], in_=abanks[j][:])
        lg = keep.tile([P, I], F32, name="lg")
        nd = keep.tile([P, I], F32, name="nd")
        ag = keep.tile([P, I], F32, name="ag")
        al = keep.tile([P, NV], F32, name="al")
        rs = keep.tile([P, I], F32, name="rs")
        r = keep.tile([P, NV], F32, name="r")
        sv, ss = slice(0, NV), slice(NV, I)
        for s in (sv, ss):
            nc.scalar.activation(lg[:, s], sg[:, s], ACT.Ln, scale=math.exp(-0.5), bias=floor[:])
        sq = rs[:, NV : 2 * NV]
        nc.vector.tensor_copy(ag[:, :H], a[:].indirect(o1[:, cols(0, H)]))
        nc.vector.tensor_tensor(nd[:, sv], nb[:, sv], lg[:, sv], ALU.min)
        nc.vector.tensor_tensor(sq, nd[:, sv], nd[:, sv], ALU.mult)
        nc.vector.tensor_tensor(nd[:, ss], nb[:, ss], lg[:, ss], ALU.min)
        nc.vector.tensor_scalar(al[:], ag[:, sv], lam_t[:], None, ALU.mult)
        nc.vector.tensor_copy(ag[:, H:], a[:].indirect(o1[:, cols(H, H)]))
        nc.scalar.activation(r[:, sv], sq, ACT.Abs_reciprocal_sqrt)
        nc.vector.tensor_tensor(f1[:].indirect(o1[:, cols(0, NV)]), al[:], r[:, sv], ALU.mult)
        nc.scalar.activation(rs[:, ss], nd[:, ss], ACT.Abs_reciprocal_sqrt)
        turned = keep.tile([P, ADD_V], F32, name="turned")
        r2 = turned[:, ADD_V - (I - NV) :]
        nc.scalar.activation(r2, rs[:, ss], ACT.Square)
        nc.scalar.activation(rs[:, ss], r2, ACT.Copy, scale=lam_t[:])
        nc.vector.tensor_tensor(f1[:].indirect(o1[:, cols(NV, I - NV)]), ag[:, ss], rs[:, ss], ALU.mult)
        f2 = keep.tile([P, T], F32, name="f2")
        pieces = ((0, 512), (512, ADD_V - 512))
        for j, (lo, n) in enumerate(pieces):
            bank = psum.tile([P, n], F32, name=f"t{j}", tag=f"a{j}")
            for c in range(0, n, P):
                nc.tensor.transpose(bank[:, c : c + P], old_t[:, lo + c : lo + c + P], ident[:])
            nc.scalar.copy(out=turned[:, lo : lo + n], in_=bank[:])
        nc.gpsimd.tensor_tensor(f2[:, ADD_V:], f1[:, ADD_V:], old_t[:, ADD_V:], ALU.add)
        for j, (lo, n) in enumerate(pieces):
            bank = psum.tile([P, n], F32, name=f"u{j}", tag=f"b{2 + j}")
            for c in range(0, n, P):
                nc.tensor.transpose(bank[:, c : c + P], turned[:, lo + c : lo + c + P], ident[:])
            nc.vector.tensor_tensor(f2[:, lo : lo + n], f1[:, lo : lo + n], bank[:], ALU.add)
        y0 = keep.tile([P, H], F32, name="y0")
        y1 = keep.tile([P, H], F32, name="y1")
        nc.vector.tensor_copy(y0[:], f2[:].indirect(o3[:, cols(0, H)]))
        nc.scalar.activation(y1[:], f2[:].indirect(o3[:, cols(H, H)]), ACT.Copy)
        nc.sync.dma_start(out=out[:, :H], in_=y0[:])
        nc.scalar.dma_start(out=out[:, H:], in_=y1[:])
